import numpy as np
import ml_dtypes


def mxq(x, axis, fmt="e4m3"):
    dtype, down = {"e4m3": (ml_dtypes.float8_e4m3fn, 7), "e5m2": (ml_dtypes.float8_e5m2, 14)}[fmt]
    v = np.moveaxis(np.asarray(x, np.float32).astype(ml_dtypes.bfloat16).astype(np.float64), axis, -1)
    blocks = v.reshape(v.shape[:-1] + (-1, 32))
    amax = np.abs(blocks).max(-1, keepdims=True)
    byte = np.maximum(np.where(amax > 0, np.frexp(amax)[1] - 1 + 127, 0) - down, 1)
    scale = np.exp2(byte - 127.0)
    codes = (blocks / scale).astype(np.float32).astype(dtype).astype(np.float64)
    return np.moveaxis((codes * scale).reshape(v.shape), -1, axis)


WIDE = False


def mx_kscale(k):
    if not WIDE:
        return np.ones(k)
    levels = np.array([10, -10, 5, -5, 0])
    if k % 512:
        return np.exp2(np.random.permutation(np.resize(levels, k // 32))).repeat(32)
    a = np.empty((k // 512, 16))
    for p in range(k // 512):
        a[p, :8] = np.random.permutation(np.resize(levels, 8))
        for g in range(8):
            far = levels[np.abs(levels - a[p, g]) >= 10]
            a[p, g + 8] = far[np.random.randint(len(far))]
    return np.exp2(a.ravel()).repeat(32)


BF16 = ml_dtypes.bfloat16


def bf(x):
    return np.asarray(x, np.float32).astype(BF16)


def f64(x):
    return np.asarray(x).astype(np.float64)

def planes(Y):
    n, m = Y.shape
    b = f64(bf(Y)).reshape(n // 32, 32, m)
    amax = np.abs(b).max(1)
    byte = np.clip(np.where(amax > 0, np.frexp(amax)[1] - 1 + 127 - 7, 1), 1, 254)
    codes = (b * np.exp2(127.0 - byte)[:, None, :]).reshape(n, m).astype(np.float32).astype(ml_dtypes.float8_e4m3fn).view(np.uint8)
    words = codes.reshape(n // 512, 128, 4, m).transpose(0, 1, 3, 2)
    return np.ascontiguousarray(words), np.ascontiguousarray(byte.astype(np.uint8).reshape(n // 512, 16, m))


ACC, CUR, SCN, MEM = 2048, 512, 1024, 512

MOVE_SPREAD, SHARE_SPREAD, SIZE_SPREAD, WEIGHT_SPREAD = 0.5, 1.5, 0.5, 0.8


def setup_inputs():
    rn = np.random.randn
    s = mx_kscale(CUR)
    t = mx_kscale(ACC)
    exposures = rn(ACC, CUR) / np.sqrt(CUR)
    moves = rn(CUR, SCN)
    margin_map = (MEM / ACC) * np.exp(MOVE_SPREAD * rn(ACC, SCN))
    raw = np.exp(SHARE_SPREAD * rn(MEM, ACC)) * np.exp(SIZE_SPREAD * rn(MEM, 1))
    shares = raw / raw.sum(axis=0, keepdims=True)
    return {
        "exposures": bf(exposures * s[None, :]),
        "moves": bf(moves / s[:, None]),
        "margin_map": bf(margin_map * t[:, None]),
        "shares": bf(shares / t[None, :]),
        "concentration": bf(1 + 0.1 * rn(MEM)),
        "addon": bf(0.3 * np.abs(rn(MEM))),
        "scenario_weights": bf(np.exp(WEIGHT_SPREAD * rn(SCN))),
    }


def reference(exposures, moves, margin_map, shares, concentration, addon, scenario_weights):
    pnl = mxq(f64(exposures), 1, "e4m3") @ mxq(f64(moves), 0, "e4m3")
    h = np.abs(pnl) * f64(margin_map)
    p = mxq(f64(shares), 1, "e4m3") @ mxq(h, 0, "e4m3")
    y = (p * f64(concentration)[:, None] + f64(addon)[:, None]) * f64(scenario_weights)[None, :]
    words, scales = planes(y.T)
    return y, words, scales

@@ -1,0 +1,403 @@
+from contextlib import ExitStack
+
+import concourse.mybir as mybir
+from concourse.masks import make_identity
+
+F32 = mybir.dt.float32
+BF16 = mybir.dt.bfloat16
+U32 = mybir.dt.uint32
+I32 = mybir.dt.int32
+U8 = mybir.dt.uint8
+FP8X4 = mybir.dt.float8_e4m3fn_x4
+ACT = mybir.ActivationFunctionType
+MULT = mybir.AluOpType.mult
+ADD = mybir.AluOpType.add
+
+ACC, CUR, SCN, MEM = 2048, 512, 1024, 512
+FLOPS = 2 * ACC * CUR * SCN + 2 * MEM * ACC * SCN
+
+P = 128
+BANK = 512
+RUN = 4
+
+CHUNKS = [512,256,128,128]
+PIECES = [[128,128,256,256,128,128],[512,256,128,128],[512,256,128,128],[512,256,128,128]]
+MOVE_PARTS = [256,256,512]
+ON_VECTOR = ["K02","K11"]
+OPEN_CHUNKS = [3]
+ABS_RING = 16
+
+ORDER_TEXT = {
+    "D": "LE0b LE0a Lmv0 Lmv1 LE1 Lmv2 LE2 Lmm00 LE3 LS0 Lmm10 Lmm20 LS1 Lmm30 LS2 Lmm21 LS3 Lmm01 Lmm31 Lmm11 So0 So1 So2 Sw0 So3 Sw2 Sw1 Sw3",
+    "P": "TE01 TE00 Tw TE11 Tc M010 M021 TE10 M000 TE21 TE20 M020 M101 M103 M031 M102 TE30 M030 M100 M203 M202 TS01 TE31 M200 M201 TS00 M110 TS10 M300 M303 M302 M301 TS11 M220 TS20 TS21 M210 M040 M111 M311 M211 TS31 M120 TS30 M320 M330 M310 M050 N01 N02 N03 N00 M130 N11 M230 N10 U03 N20 U01 U00 U02 U10 U11 N30a N31a N31 N30 N32a N32 N33a N33 U20 U30",
+    "A": "CE01 CE00 Cw CE11 A010 Cc A021 CE10 A000 CE21 CE20 A101 A020 A102 A103 A100 CE30 A203 CE31 A201 A202 A200 CS00 CS01 A300 A303 A302 A301 CS11 CS10 A030 CS21 A031 A111 A210 A110 CS20 CS31 CS30 A211 A320 A311 A220 A310 A120 F01 A330 A050 A040 F03 A130 F00 F12 F13 F02 A230 K03 F10 F11 F20 F21 K01 F22 F23 K00 K10 F31 F30 F32 F33 K20 K30",
+    "V": "I0 I1 QE0 Qm0 Qm1 I2 Qm2 QE1 H01 H00 QE2 Qh00 Qh01 H02 Qh02 H10 QE3 Qh10 H20 QS0 Qh20 H30 QS1 H03 Qh30 H11 QS2 Qh03 QS3 Qh11 H32 H21 H22 H31 Qh21 Qh31 Y01 H12 H04 Qh22 Y03 Qh12 Y00 Qh04 Qh32 H13 Y02 H33 H05 Y11 Y10 H23 Qh13 Qh23 Qh05 Qh33 Y20 K02 Qy0 Y30 K11 Qy2 Qy1 Qy3",
+}
+
+
+def starts(widths):
+    return [sum(widths[:k]) for k in range(len(widths))]
+
+
+def tile_fx_member_margin_planes_h3_kernel(
+    tc, exposures, moves, margin_map, shares, concentration, addon, scenario_weights, out_0, out_1, out_2
+):
+    nc = tc.nc
+    ORDER = {engine: text.split() for engine, text in ORDER_TEXT.items()}
+    with ExitStack() as ctx:
+        sb = ctx.enter_context(tc.tile_pool(name="sb", bufs=1))
+        ps = ctx.enter_context(tc.psum_pool(name="ps", bufs=1))
+        ctx.enter_context(tc.manual_schedule())
+
+        def new(name, shape, dtype):
+            return sb.tile(shape, dtype, name=name, align_bytes=64)
+
+        banks = [ps.tile([P, BANK], F32, name="bank%d" % b) for b in range(8)]
+        free_banks = list(range(8))
+        bank_of = {}
+        steps = {}
+
+        def step(name, needs, run, takes_bank=False, frees=None):
+            steps[name] = (needs, run, takes_bank, frees)
+
+        def copy_on(name, out, in_):
+            if name in ON_VECTOR:
+                nc.vector.tensor_copy(out=out, in_=in_)
+            else:
+                nc.scalar.copy(out=out, in_=in_)
+
+        def quantize(codes, scales, grouped):
+            nc.vector.quantize_mx(out=codes.bitcast(FP8X4), scales=scales, in_=grouped)
+
+        ident = new("ident", [P, P], F32)
+        vec_rows = new("vec_rows", [8, P], BF16)
+        vec_f32 = new("vec_f32", [P, P], F32)
+        w_cols = new("w_cols", [P, 8], BF16)
+        w_row = new("w_row", [P, SCN], BF16)
+        member = new("member", [P, 8], F32)
+
+        make_identity(nc, ident[:])
+        nc.gpsimd.memset(vec_f32[:], 0.0)
+        nc.scalar.dma_start(out=vec_rows[0:4, :], in_=concentration.rearrange("(i m) -> i m", m=P))
+        nc.scalar.dma_start(out=vec_rows[4:8, :], in_=addon.rearrange("(i m) -> i m", m=P))
+        nc.scalar.dma_start(out=w_cols[:], in_=scenario_weights.rearrange("(n j) -> n j", j=8))
+        nc.scalar.activation(out=vec_f32[0:8, :], in_=vec_rows[:], func=ACT.Identity)
+
+        def turn_member():
+            nc.tensor.transpose(banks[bank_of["Tc"]][:, 0:P], vec_f32[:], ident[:])
+
+        def copy_member():
+            nc.scalar.copy(out=member[:], in_=banks[bank_of["Tc"]][:, 0:8])
+
+        def turn_weights():
+            words = w_cols[:].bitcast(F32)
+            for j in range(4):
+                nc.tensor.transpose(
+                    banks[bank_of["Tw"]][:, j * P : (j + 1) * P], words[:, j : j + 1].to_broadcast([P, P]), ident[:]
+                )
+
+        def copy_weights():
+            copy_on("Cw", w_row[:].bitcast(F32).rearrange("p (n j) -> p n j", j=4),
+                    banks[bank_of["Tw"]][:].rearrange("p (j n) -> p n j", j=4))
+
+        step("Tc", [], turn_member, takes_bank=True)
+        step("Cc", ["Tc"], copy_member, frees="Tc")
+        step("Tw", [], turn_weights, takes_bank=True)
+        step("Cw", ["Tw"], copy_weights, frees="Tw")
+
+        codes = {}
+        scales = {}
+        turned = [new("turned%d" % k, [P, 4 * BANK], BF16) for k in range(4)]
+
+        def add_turned_operand(op, g):
+            key = "%s%d" % (op, g)
+            raw = new("raw" + key, [P, 4, BANK], BF16)
+            grouped = turned[g]
+            codes[key] = new("codes" + key, [P, BANK], U32)
+            scales[key] = new("scales" + key, [P, BANK], U8)
+            if op == "E":
+                source = exposures[BANK * g : BANK * (g + 1), :].rearrange("(m t) k -> m t k", t=4)
+            else:
+                source = shares[:, BANK * g : BANK * (g + 1)].rearrange("(i m) k -> m i k", m=P)
+            if key == "E0":
+                step("LE0a", [], lambda: nc.sync.dma_start(out=raw[:, 0:2, :], in_=source[:, 0:2, :]))
+                step("LE0b", [], lambda: nc.sync.dma_start(out=raw[:, 2:4, :], in_=source[:, 2:4, :]))
+            else:
+                step("L" + key, [], lambda: nc.sync.dma_start(out=raw[:], in_=source))
+
+            def add_half(h):
+                name = "T%s%d" % (key, h)
+
+                def turn():
+                    words = raw[:].bitcast(F32)
+                    for j in range(2):
+                        for u in range(2):
+                            q = 2 * j + u
+                            nc.tensor.transpose(
+                                banks[bank_of[name]][:, q * P : (q + 1) * P], words[:, 2 * h + j, u:256:2], ident[:]
+                            )
+
+                def copy():
+                    out = grouped[:].bitcast(F32)[:, BANK * h : BANK * (h + 1)]
+                    copy_on("C%s%d" % (key, h), out.rearrange("p (j m u) -> p j m u", j=2, u=2),
+                            banks[bank_of[name]][:].rearrange("p (j u m) -> p j m u", j=2, u=2))
+
+                load = "LE0" + "ab"[h] if key == "E0" else "L" + key
+                step(name, [load], turn, takes_bank=True)
+                step("C%s%d" % (key, h), [name] + (["QE%d" % g] if op == "S" else []), copy, frees=name)
+
+            add_half(0)
+            add_half(1)
+            step("Q" + key, ["C%s0" % key, "C%s1" % key], lambda: quantize(codes[key][:], scales[key][:], grouped[:]))
+
+        for op in "ES":
+            for g in range(4):
+                add_turned_operand(op, g)
+
+        move_codes = new("move_codes", [P, SCN], U32)
+        move_scales = new("move_scales", [P, SCN], U8)
+
+        def add_moves(h, s0, width):
+            raw = new("move_raw%d" % h, [P, 4, width], BF16)
+            grouped = new("move_grouped%d" % h, [P, 4 * width], BF16)
+            source = moves[:, s0 : s0 + width].rearrange("(p t) n -> p t n", t=4)
+            step("Lmv%d" % h, [], lambda: nc.sync.dma_start(out=raw[:], in_=source))
+            step("I%d" % h, ["Lmv%d" % h], lambda: copy_on(
+                "I%d" % h,
+                grouped[:].rearrange("p (c i t) -> p c t i", i=4, t=4),
+                raw[:].rearrange("p t (c i) -> p c t i", i=4)))
+            step("Qm%d" % h, ["I%d" % h], lambda: quantize(
+                move_codes[:, s0 : s0 + width], move_scales[:, s0 : s0 + width], grouped[:]))
+
+        for h, (s0, width) in enumerate(zip(starts(MOVE_PARTS), MOVE_PARTS)):
+            add_moves(h, s0, width)
+
+        maps = {}
+
+        def add_map(g, h):
+            maps[g, h] = new("map%d%d" % (g, h), [P, 4, BANK], BF16)
+            source = margin_map[BANK * g : BANK * (g + 1), BANK * h : BANK * (h + 1)].rearrange("(p t) n -> p t n", t=4)
+            step("Lmm%d%d" % (g, h), [], lambda: nc.sync.dma_start(out=maps[g, h][:], in_=source))
+
+        for g in range(4):
+            for h in range(2):
+                add_map(g, h)
+
+        def covering(prefix, widths, s0, width):
+            return [prefix + str(k) for k, (a, w) in enumerate(zip(starts(widths), widths)) if a < s0 + width and a + w > s0]
+
+        h_codes = [new("h_codes%d" % g, [P, SCN], U32) for g in range(4)]
+        h_scales = [new("h_scales%d" % g, [P, SCN], U8) for g in range(4)]
+
+        h_order = [name for name in ORDER["V"] if name[0] == "H"]
+        slot_user = {}
+        size_ring = new("size_ring", [P, ABS_RING * BANK], F32)
+        h_ring = new("h_ring", [P, ABS_RING * BANK], BF16)
+        ring_at = {}
+        ring_needs = {}
+        cursor = 0
+        for name in h_order:
+            nb = 4 * PIECES[int(name[1])][int(name[2])] // BANK
+            if cursor + nb > ABS_RING:
+                cursor = 0
+            ring_at[name] = cursor
+            ring_needs[name] = sorted(set(slot_user[s] for s in range(cursor, cursor + nb) if s in slot_user))
+            for s in range(cursor, cursor + nb):
+                slot_user[s] = name
+            cursor = cursor + nb
+
+        def add_piece(g, c, s0, width):
+            nb = 4 * width // BANK
+            per = BANK // width
+            key = "%d%d" % (g, c)
+            at = ring_at["H" + key] * BANK
+            size = size_ring[:, at : at + 4 * width]
+            grouped = h_ring[:, at : at + 4 * width]
+            cols = slice(s0, s0 + width)
+
+            def add_bank(b):
+                name = "M%s%d" % (key, b)
+
+                def multiply():
+                    for j in range(per):
+                        t = b * per + j
+                        nc.tensor.matmul_mx(
+                            out=banks[bank_of[name]][:, j * width : (j + 1) * width],
+                            lhsT=codes["E%d" % g][:, t * P : (t + 1) * P].bitcast(FP8X4),
+                            lhsT_scale=scales["E%d" % g][:, t * P : (t + 1) * P],
+                            rhs=move_codes[:, cols].bitcast(FP8X4),
+                            rhs_scale=move_scales[:, cols],
+                            start=True,
+                            stop=True,
+                        )
+
+                step(name, ["QE%d" % g] + covering("Qm", MOVE_PARTS, s0, width), multiply, takes_bank=True)
+                step("A%s%d" % (key, b), [name] + ring_needs["H" + key], lambda: nc.scalar.activation(
+                    out=size[:, b * BANK : (b + 1) * BANK], in_=banks[bank_of[name]][:], func=ACT.Abs), frees=name)
+
+            for b in range(nb):
+                add_bank(b)
+            half, n0 = divmod(s0, BANK)
+            step("H" + key,
+                 ["A%s%d" % (key, b) for b in range(nb)] + ["Lmm%d%d" % (g, half)]
+                 + ["Qh" + u[1:] for u in ring_needs["H" + key]],
+                 lambda: nc.vector.tensor_tensor(
+                     out=grouped.rearrange("p (c i t) -> p c t i", i=RUN, t=4),
+                     in0=size.rearrange("p (t c i) -> p c t i", i=RUN, t=4),
+                     in1=maps[g, half][:, :, n0 : n0 + width].rearrange("p t (c i) -> p c t i", i=RUN),
+                     op=MULT))
+            step("Qh" + key, ["H" + key], lambda: quantize(h_codes[g][:, cols], h_scales[g][:, cols], grouped))
+
+        for g in range(4):
+            for c, (s0, width) in enumerate(zip(starts(PIECES[g]), PIECES[g])):
+                add_piece(g, c, s0, width)
+
+        out_words = out_1.rearrange("g p m t -> g p (m t)").bitcast(I32)
+        out_scales = out_2.bitcast(I32)
+
+        def add_chunk(c, s0, width):
+            nb = 4 * width // BANK
+            per = BANK // width
+            cols = slice(s0, s0 + width)
+            last = c == len(CHUNKS) - 1
+            y = new("y%d" % c, [P, 4 * width], F32)
+            y_grouped = new("y_grouped%d" % c, [P, 4 * width], BF16)
+            y_codes = new("y_codes%d" % c, [P, width], U32)
+            y_scales = new("y_scales%d" % c, [P, width], U8)
+
+            def ready(g):
+                return covering("Qh%d" % g, PIECES[g], s0, width) + ["QS%d" % g]
+
+            def passes(owner, j, i, groups):
+                for g in groups:
+                    nc.tensor.matmul_mx(
+                        out=banks[bank_of[owner]][:, j * width : (j + 1) * width],
+                        lhsT=codes["S%d" % g][:, i * P : (i + 1) * P].bitcast(FP8X4),
+                        lhsT_scale=scales["S%d" % g][:, i * P : (i + 1) * P],
+                        rhs=h_codes[g][:, cols].bitcast(FP8X4),
+                        rhs_scale=h_scales[g][:, cols],
+                        start=(g == 0),
+                        stop=(g == 3),
+                    )
+
+            def add_affine(owner, needs, j, i, frees):
+                name = "F%d%d" % (c, i)
+                out = y[:, i * width : (i + 1) * width]
+
+                def run():
+                    in_ = banks[bank_of[owner]][:, j * width : (j + 1) * width]
+                    if name in ON_VECTOR:
+                        nc.vector.tensor_scalar(out=out, in0=in_, scalar1=member[:, i : i + 1],
+                                                scalar2=member[:, 4 + i : 5 + i], op0=MULT, op1=ADD)
+                    else:
+                        nc.scalar.activation(out=out, in_=in_, func=ACT.Identity,
+                                             scale=member[:, i : i + 1], bias=member[:, 4 + i : 5 + i])
+
+                step(name, needs + ["Cc"], run, frees=frees)
+
+            def add_open_group(i):
+                owner = "N%d%da" % (c, i)
+                step(owner, ready(0) + ready(1) + ready(2), lambda: passes(owner, 0, i, range(3)), takes_bank=True)
+                step(owner[:-1], [owner] + ready(3), lambda: passes(owner, 0, i, [3]))
+                add_affine(owner, [owner[:-1]], 0, i, owner)
+
+            def add_closed_groups(b):
+                owner = "N%d%d" % (c, b)
+
+                def run():
+                    for j in range(per):
+                        passes(owner, j, b * per + j, range(4))
+
+                step(owner, ready(0) + ready(1) + ready(2) + ready(3), run, takes_bank=True)
+                names = [name for name in ORDER["A"] + ORDER["V"]
+                         if name in ["F%d%d" % (c, b * per + j) for j in range(per)]]
+                for j in range(per):
+                    i = b * per + j
+                    is_last = names[-1] == "F%d%d" % (c, i)
+                    add_affine(owner, [owner] + (names[:-1] if is_last else []), j, i, owner if is_last else None)
+
+            def add_bank(b):
+                span = slice(b * BANK, (b + 1) * BANK)
+                name = "U%d%d" % (c, b)
+
+                def weigh():
+                    nc.vector.tensor_tensor(
+                        out=y[:, span].rearrange("p (j n) -> p j n", j=per),
+                        in0=y[:, span].rearrange("p (j n) -> p j n", j=per),
+                        in1=w_row[:, cols].unsqueeze(1).to_broadcast([P, per, width]),
+                        op=MULT)
+
+                def turn():
+                    for t in range(4):
+                        nc.tensor.transpose(
+                            banks[bank_of[name]][:, t * P : (t + 1) * P],
+                            y[:, b * BANK + t : (b + 1) * BANK : 4], ident[:])
+
+                step("Y%d%d" % (c, b), ["F%d%d" % (c, b * per + j) for j in range(per)] + ["Cw"], weigh)
+                step(name, ["Y%d%d" % (c, b)], turn, takes_bank=True)
+                step("K%d%d" % (c, b), [name], lambda: copy_on(
+                    "K%d%d" % (c, b),
+                    y_grouped[:, span].rearrange("p (m t) -> p m t", t=4),
+                    banks[bank_of[name]][:].rearrange("p (t m) -> p m t", t=4)), frees=name)
+
+            if c in OPEN_CHUNKS:
+                for i in range(4):
+                    add_open_group(i)
+            else:
+                for b in range(nb):
+                    add_closed_groups(b)
+            for b in range(nb):
+                add_bank(b)
+            step("Qy%d" % c, ["K%d%d" % (c, b) for b in range(nb)],
+                 lambda: quantize(y_codes[:], y_scales[:], y_grouped[:]))
+
+            def store_y():
+                nc.sync.dma_start(out=out_0[:, cols].rearrange("(i m) s -> m i s", m=P),
+                                  in_=y[:].rearrange("p (i s) -> p i s", i=4))
+
+            def store_planes():
+                group, n0 = divmod(s0, BANK)
+                rows = width // 4
+                blocks = width // 32
+                words = out_words[group, n0 // 4 : n0 // 4 + rows, :].rearrange("j (b e m) -> j e b m", e=per, m=P)
+                for e in range(per):
+                    nc.sync.dma_start(
+                        out=words[:, e, :, :],
+                        in_=y_codes[e * rows : (e + 1) * rows, :].bitcast(I32).rearrange("p (b m) -> p b m", m=P))
+                scale_queue = nc.scalar if last else nc.sync
+                for quad in range(4):
+                    e, local = divmod(4 * quad, blocks)
+                    q0 = n0 // 32 + local
+                    rows4 = out_scales[group, q0 : q0 + 4, :].rearrange("r (b e m) -> r e b m", e=per, m=P // 4)
+                    scale_queue.dma_start(
+                        out=rows4[:, e, :, :],
+                        in_=y_scales[32 * quad : 32 * quad + 4, :].bitcast(I32).rearrange("p (b m) -> p b m", m=P // 4))
+
+            step("So%d" % c, ["Y%d%d" % (c, b) for b in range(nb)], store_y)
+            step("Sw%d" % c, ["Qy%d" % c] + (ORDER["A"][-1:] if last else []), store_planes)
+
+        for c, (s0, width) in enumerate(zip(starts(CHUNKS), CHUNKS)):
+            add_chunk(c, s0, width)
+
+        done = set()
+        at = {engine: 0 for engine in ORDER}
+        assert sorted(steps) == sorted(name for names in ORDER.values() for name in names)
+        while len(done) < len(steps):
+            moved = False
+            for engine in "DPVA":
+                if at[engine] == len(ORDER[engine]):
+                    continue
+                name = ORDER[engine][at[engine]]
+                needs, run, takes_bank, frees = steps[name]
+                if not all(need in done for need in needs) or (takes_bank and not free_banks):
+                    continue
+                if takes_bank:
+                    bank_of[name] = free_banks.pop(0)
+                run()
+                if frees:
+                    free_banks.append(bank_of[frees])
+                done.add(name)
+                at[engine] = at[engine] + 1
+                moved = True
+                break
+            assert moved

@@ -23,15 +23,17 @@ RUN = 4
 CHUNKS = [512,256,128,128]
 PIECES = [[128,128,256,256,128,128],[512,256,128,128],[512,256,128,128],[512,256,128,128]]
 MOVE_PARTS = [256,256,512]
-ON_VECTOR = ["K02","K11"]
+GROUPS = [2,2,2,1,1]
+WORD_BATCHES = [[0,1,2],[3,4]]
+WARM = 0
 OPEN_CHUNKS = [3]
 ABS_RING = 16
 
 ORDER_TEXT = {
-    "D": "LE0b LE0a Lmv0 Lmv1 LE1 Lmv2 LE2 Lmm00 LE3 LS0 Lmm10 Lmm20 LS1 Lmm30 LS2 Lmm21 LS3 Lmm01 Lmm31 Lmm11 So0 So1 So2 Sw0 So3 Sw2 Sw1 Sw3",
-    "P": "TE01 TE00 Tw TE11 Tc M010 M021 TE10 M000 TE21 TE20 M020 M101 M103 M031 M102 TE30 M030 M100 M203 M202 TS01 TE31 M200 M201 TS00 M110 TS10 M300 M303 M302 M301 TS11 M220 TS20 TS21 M210 M040 M111 M311 M211 TS31 M120 TS30 M320 M330 M310 M050 N01 N02 N03 N00 M130 N11 M230 N10 U03 N20 U01 U00 U02 U10 U11 N30a N31a N31 N30 N32a N32 N33a N33 U20 U30",
-    "A": "CE01 CE00 Cw CE11 A010 Cc A021 CE10 A000 CE21 CE20 A101 A020 A102 A103 A100 CE30 A203 CE31 A201 A202 A200 CS00 CS01 A300 A303 A302 A301 CS11 CS10 A030 CS21 A031 A111 A210 A110 CS20 CS31 CS30 A211 A320 A311 A220 A310 A120 F01 A330 A050 A040 F03 A130 F00 F12 F13 F02 A230 K03 F10 F11 F20 F21 K01 F22 F23 K00 K10 F31 F30 F32 F33 K20 K30",
-    "V": "I0 I1 QE0 Qm0 Qm1 I2 Qm2 QE1 H01 H00 QE2 Qh00 Qh01 H02 Qh02 H10 QE3 Qh10 H20 QS0 Qh20 H30 QS1 H03 Qh30 H11 QS2 Qh03 QS3 Qh11 H32 H21 H22 H31 Qh21 Qh31 Y01 H12 H04 Qh22 Y03 Qh12 Y00 Qh04 Qh32 H13 Y02 H33 H05 Y11 Y10 H23 Qh13 Qh23 Qh05 Qh33 Y20 K02 Qy0 Y30 K11 Qy2 Qy1 Qy3",
+    "D": "LE0a LE0b Lmv0 LE1 Lmv1 Lmv2 LE2 Lmm00 LE3 Lmm10 LS2 LS0 Lmm20 LS1 LS3 Cw Lmm30 Lmm01 Lmm31 Lmm11 Lmm21 So0 So1 So2 So5 So3 So4 So6 Sw00 Sw03 Sw02 So7 Sw01 Sw12 Ss1 Sw13 Ss2 Sw10 Ss3 Sw11 Ss0",
+    "P": "TE00 TE01 Tc TE10 TE11 M010 M000 M021 M020 TE20 TE21 M103 M100 M101 TE30 M102 M120 TE31 TS20 M203 M202 M200 M201 TS01 TS00 TS21 M303 M302 M300 TS10 M301 M030 TS30 TS11 M031 M210 M211 TS31 M310 M111 M110 M220 M230 M311 M040 N03 M320 N00 N01 M050 M330 M130 N02 N11 N10 N20 U1 U2 U0 N32a N30a N33a N31a N31 N30 N33 N32 U3 U4",
+    "A": "CE00 CE01 CE10 Cc CE11 A010 A000 A021 CE20 A020 CE21 A101 A103 A100 A102 CE31 CE30 A200 A203 A201 A202 CS01 CS00 A300 A302 A303 A301 A030 CS20 A031 CS21 CS30 CS31 CS11 CS10 A111 A110 A210 A211 A310 A040 A220 A120 A311 F00 A320 F01 A050 F03 F02 A330 F12 A130 F10 F11 F13 A230 F20 F21 B1 B0 K1 F22 F23 K2 K0 F31 F30 F33 F32 K3 K4",
+    "V": "I0 Qm0 QE0 I1 Qm1 I2 QE1 Qm2 H00 Qh00 H02 QE2 H01 Qh02 Qh01 H10 QE3 Qh10 H20 QS0 Qh20 H30 H03 Qh30 QS2 QS1 QS3 H11 Qh03 Qh11 H21 H04 Qh21 H12 H31 Qh12 Qh31 H32 H05 Qh04 H22 Qh32 Qh22 Qh05 Y0 Y1 H23 Y2 H13 B2 Qh13 Qh23 H33 Y3 Qh33 Qy2 Qy1 Qy0 B3 Y4 B4 Qy3 Qy4",
 }
 
 
@@ -61,7 +63,7 @@ def tile_fx_member_margin_planes_h3_kernel(
             steps[name] = (needs, run, takes_bank, frees)
 
         def copy_on(name, out, in_):
-            if name in ON_VECTOR:
+            if name in ORDER["V"]:
                 nc.vector.tensor_copy(out=out, in_=in_)
             else:
                 nc.scalar.copy(out=out, in_=in_)
@@ -72,7 +74,6 @@ def tile_fx_member_margin_planes_h3_kernel(
         ident = new("ident", [P, P], F32)
         vec_rows = new("vec_rows", [8, P], BF16)
         vec_f32 = new("vec_f32", [P, P], F32)
-        w_cols = new("w_cols", [P, 8], BF16)
         w_row = new("w_row", [P, SCN], BF16)
         member = new("member", [P, 8], F32)
 
@@ -80,7 +81,6 @@ def tile_fx_member_margin_planes_h3_kernel(
         nc.gpsimd.memset(vec_f32[:], 0.0)
         nc.scalar.dma_start(out=vec_rows[0:4, :], in_=concentration.rearrange("(i m) -> i m", m=P))
         nc.scalar.dma_start(out=vec_rows[4:8, :], in_=addon.rearrange("(i m) -> i m", m=P))
-        nc.scalar.dma_start(out=w_cols[:], in_=scenario_weights.rearrange("(n j) -> n j", j=8))
         nc.scalar.activation(out=vec_f32[0:8, :], in_=vec_rows[:], func=ACT.Identity)
 
         def turn_member():
@@ -89,21 +89,9 @@ def tile_fx_member_margin_planes_h3_kernel(
         def copy_member():
             nc.scalar.copy(out=member[:], in_=banks[bank_of["Tc"]][:, 0:8])
 
-        def turn_weights():
-            words = w_cols[:].bitcast(F32)
-            for j in range(4):
-                nc.tensor.transpose(
-                    banks[bank_of["Tw"]][:, j * P : (j + 1) * P], words[:, j : j + 1].to_broadcast([P, P]), ident[:]
-                )
-
-        def copy_weights():
-            copy_on("Cw", w_row[:].bitcast(F32).rearrange("p (n j) -> p n j", j=4),
-                    banks[bank_of["Tw"]][:].rearrange("p (j n) -> p n j", j=4))
-
         step("Tc", [], turn_member, takes_bank=True)
         step("Cc", ["Tc"], copy_member, frees="Tc")
-        step("Tw", [], turn_weights, takes_bank=True)
-        step("Cw", ["Tw"], copy_weights, frees="Tw")
+        step("Cw", [], lambda: nc.sync.dma_start(out=w_row[:], in_=scenario_weights.partition_broadcast(P)))
 
         codes = {}
         scales = {}
@@ -252,18 +240,14 @@ def tile_fx_member_margin_planes_h3_kernel(
             for c, (s0, width) in enumerate(zip(starts(PIECES[g]), PIECES[g])):
                 add_piece(g, c, s0, width)
 
-        out_words = out_1.rearrange("g p m t -> g p (m t)").bitcast(I32)
-        out_scales = out_2.bitcast(I32)
+        y = new("y", [P, 8, 4, P], F32)
+        y_codes = new("y_codes", [P, SCN], U32)
+        y_scales = new("y_scales", [P, SCN], U8)
 
         def add_chunk(c, s0, width):
             nb = 4 * width // BANK
             per = BANK // width
             cols = slice(s0, s0 + width)
-            last = c == len(CHUNKS) - 1
-            y = new("y%d" % c, [P, 4 * width], F32)
-            y_grouped = new("y_grouped%d" % c, [P, 4 * width], BF16)
-            y_codes = new("y_codes%d" % c, [P, width], U32)
-            y_scales = new("y_scales%d" % c, [P, width], U8)
 
             def ready(g):
                 return covering("Qh%d" % g, PIECES[g], s0, width) + ["QS%d" % g]
@@ -282,11 +266,11 @@ def tile_fx_member_margin_planes_h3_kernel(
 
             def add_affine(owner, needs, j, i, frees):
                 name = "F%d%d" % (c, i)
-                out = y[:, i * width : (i + 1) * width]
+                out = y[:, s0 // P : (s0 + width) // P, i, :]
 
                 def run():
-                    in_ = banks[bank_of[owner]][:, j * width : (j + 1) * width]
-                    if name in ON_VECTOR:
+                    in_ = banks[bank_of[owner]][:, j * width : (j + 1) * width].rearrange("p (k n) -> p k n", n=P)
+                    if name in ORDER["V"]:
                         nc.vector.tensor_scalar(out=out, in0=in_, scalar1=member[:, i : i + 1],
                                                 scalar2=member[:, 4 + i : 5 + i], op0=MULT, op1=ADD)
                     else:
@@ -316,68 +300,73 @@ def tile_fx_member_margin_planes_h3_kernel(
                     is_last = names[-1] == "F%d%d" % (c, i)
                     add_affine(owner, [owner] + (names[:-1] if is_last else []), j, i, owner if is_last else None)
 
-            def add_bank(b):
-                span = slice(b * BANK, (b + 1) * BANK)
-                name = "U%d%d" % (c, b)
-
-                def weigh():
-                    nc.vector.tensor_tensor(
-                        out=y[:, span].rearrange("p (j n) -> p j n", j=per),
-                        in0=y[:, span].rearrange("p (j n) -> p j n", j=per),
-                        in1=w_row[:, cols].unsqueeze(1).to_broadcast([P, per, width]),
-                        op=MULT)
-
-                def turn():
-                    for t in range(4):
-                        nc.tensor.transpose(
-                            banks[bank_of[name]][:, t * P : (t + 1) * P],
-                            y[:, b * BANK + t : (b + 1) * BANK : 4], ident[:])
-
-                step("Y%d%d" % (c, b), ["F%d%d" % (c, b * per + j) for j in range(per)] + ["Cw"], weigh)
-                step(name, ["Y%d%d" % (c, b)], turn, takes_bank=True)
-                step("K%d%d" % (c, b), [name], lambda: copy_on(
-                    "K%d%d" % (c, b),
-                    y_grouped[:, span].rearrange("p (m t) -> p m t", t=4),
-                    banks[bank_of[name]][:].rearrange("p (t m) -> p m t", t=4)), frees=name)
-
             if c in OPEN_CHUNKS:
                 for i in range(4):
                     add_open_group(i)
             else:
                 for b in range(nb):
                     add_closed_groups(b)
-            for b in range(nb):
-                add_bank(b)
-            step("Qy%d" % c, ["K%d%d" % (c, b) for b in range(nb)],
-                 lambda: quantize(y_codes[:], y_scales[:], y_grouped[:]))
-
-            def store_y():
-                nc.sync.dma_start(out=out_0[:, cols].rearrange("(i m) s -> m i s", m=P),
-                                  in_=y[:].rearrange("p (i s) -> p i s", i=4))
-
-            def store_planes():
-                group, n0 = divmod(s0, BANK)
-                rows = width // 4
-                blocks = width // 32
-                words = out_words[group, n0 // 4 : n0 // 4 + rows, :].rearrange("j (b e m) -> j e b m", e=per, m=P)
-                for e in range(per):
-                    nc.sync.dma_start(
-                        out=words[:, e, :, :],
-                        in_=y_codes[e * rows : (e + 1) * rows, :].bitcast(I32).rearrange("p (b m) -> p b m", m=P))
-                scale_queue = nc.scalar if last else nc.sync
-                for quad in range(4):
-                    e, local = divmod(4 * quad, blocks)
-                    q0 = n0 // 32 + local
-                    rows4 = out_scales[group, q0 : q0 + 4, :].rearrange("r (b e m) -> r e b m", e=per, m=P // 4)
-                    scale_queue.dma_start(
-                        out=rows4[:, e, :, :],
-                        in_=y_scales[32 * quad : 32 * quad + 4, :].bitcast(I32).rearrange("p (b m) -> p b m", m=P // 4))
-
-            step("So%d" % c, ["Y%d%d" % (c, b) for b in range(nb)], store_y)
-            step("Sw%d" % c, ["Qy%d" % c] + (ORDER["A"][-1:] if last else []), store_planes)
 
         for c, (s0, width) in enumerate(zip(starts(CHUNKS), CHUNKS)):
             add_chunk(c, s0, width)
+
+        def add_group(e, k0, n):
+            part = y[:, k0 : k0 + n, :, :]
+            rounded = new("rounded%d" % e, [P, n * BANK], BF16)
+            grouped = new("y_grouped%d" % e, [P, n * BANK], BF16)
+            cols = slice(k0 * P, (k0 + n) * P)
+            name = "U%d" % e
+            weights = w_row[:, cols].rearrange("p (k n) -> p k n", n=P).unsqueeze(2).to_broadcast([P, n, 4, P])
+
+            def turn():
+                words = rounded[:].bitcast(F32).rearrange("p (u k j) -> p u k j", u=2, j=P)
+                for k in range(n):
+                    for u in range(2):
+                        q = 2 * k + u
+                        nc.tensor.transpose(banks[bank_of[name]][:, q * P : (q + 1) * P], words[:, u, k, :], ident[:])
+
+            affine = [f + str(i) for f in covering("F", CHUNKS, k0 * P, n * P) for i in range(4)]
+            step("Y%d" % e, affine + ["Cw"], lambda: nc.vector.tensor_tensor(out=part, in0=part, in1=weights, op=MULT))
+            step("B%d" % e, ["Y%d" % e], lambda: copy_on(
+                "B%d" % e,
+                rounded[:].rearrange("p (u j e) -> p u j e", u=2, e=2),
+                part.rearrange("p k i (j u e) -> p u (k i j) e", u=2, e=2)))
+            step(name, ["B%d" % e], turn, takes_bank=True)
+            step("K%d" % e, [name], lambda: copy_on(
+                "K%d" % e,
+                grouped[:].bitcast(F32).rearrange("p (k m u) -> p k m u", u=2, m=P),
+                banks[bank_of[name]][:, 0 : n * 2 * P].rearrange("p (k u m) -> p k m u", u=2, m=P)), frees=name)
+            step("Qy%d" % e, ["K%d" % e], lambda: quantize(y_codes[:, cols], y_scales[:, cols], grouped[:]))
+
+            def add_store(k):
+                step("So%d" % k, ["Y%d" % e], lambda: nc.sync.dma_start(
+                    out=out_0[:, k * P : (k + 1) * P].rearrange("(i m) s -> m i s", m=P), in_=y[:, k, :, :]))
+
+            for k in range(k0, k0 + n):
+                add_store(k)
+
+        for e, (k0, n) in enumerate(zip(starts(GROUPS), GROUPS)):
+            add_group(e, k0, n)
+
+        out_words = out_1.rearrange("g (c j) (i m) t -> j i (g c) (m t)", j=32, m=P).bitcast(I32)
+        out_scales = out_2.rearrange("g (c r) (i m) -> r i (g c) m", r=4, m=P).bitcast(I32)
+
+        def add_word_store(b, groups, i):
+            k0 = starts(GROUPS)[groups[0]]
+            k1 = k0 + sum(GROUPS[e] for e in groups)
+            step("Sw%d%d" % (b, i), ["Qy%d" % e for e in groups], lambda: nc.sync.dma_start(
+                out=out_words[:, i, k0:k1, :],
+                in_=y_codes[32 * i : 32 * i + 32, k0 * P : k1 * P].bitcast(I32).rearrange("p (k m) -> p k m", m=P)))
+
+        def add_scale_store(i):
+            step("Ss%d" % i, ["Qy%d" % e for e in range(len(GROUPS))] + ORDER["A"][-1:], lambda: nc.scalar.dma_start(
+                out=out_scales[:, i, :, :],
+                in_=y_scales[32 * i : 32 * i + 4, :].bitcast(I32).rearrange("p (k m) -> p k m", m=P // 4)))
+
+        for i in range(4):
+            for b, groups in enumerate(WORD_BATCHES):
+                add_word_store(b, groups, i)
+            add_scale_store(i)
 
         done = set()
         at = {engine: 0 for engine in ORDER}

@@ -17,35 +17,61 @@ ACC, CUR, SCN, MEM = 2048, 512, 1024, 512
 FLOPS = 2 * ACC * CUR * SCN + 2 * MEM * ACC * SCN
 
 P = 128
+PACK = 4
 BANK = 512
-RUN = 4
+BANKS = 8
+PASSES = ACC // BANK
+TILES = MEM // P
+HALVES = SCN // BANK
+QUADRANT = 32
 
-CHUNKS = [512,256,128,128]
-PIECES = [[128,128,256,256,128,128],[512,256,128,128],[512,256,128,128],[512,256,128,128]]
-MOVE_PARTS = [256,256,512]
-GROUPS = [2,2,2,1,1]
-WORD_BATCHES = [[0,1,2],[3,4]]
-WARM = 0
-OPEN_CHUNKS = [3]
-ABS_RING = 16
+H_RUN = 2
+MOVES_RUN = 4
 
-ORDER_TEXT = {
-    "D": "LE0a LE0b Lmv0 LE1 Lmv1 Lmv2 LE2 Lmm00 LE3 Lmm10 LS2 LS0 Lmm20 LS1 LS3 Cw Lmm30 Lmm01 Lmm31 Lmm11 Lmm21 So0 So1 So2 So5 So3 So4 So6 Sw00 Sw03 Sw02 So7 Sw01 Sw12 Ss1 Sw13 Ss2 Sw10 Ss3 Sw11 Ss0",
-    "P": "TE00 TE01 Tc TE10 TE11 M010 M000 M021 M020 TE20 TE21 M103 M100 M101 TE30 M102 M120 TE31 TS20 M203 M202 M200 M201 TS01 TS00 TS21 M303 M302 M300 TS10 M301 M030 TS30 TS11 M031 M210 M211 TS31 M310 M111 M110 M220 M230 M311 M040 N03 M320 N00 N01 M050 M330 M130 N02 N11 N10 N20 U1 U2 U0 N32a N30a N33a N31a N31 N30 N33 N32 U3 U4",
-    "A": "CE00 CE01 CE10 Cc CE11 A010 A000 A021 CE20 A020 CE21 A101 A103 A100 A102 CE31 CE30 A200 A203 A201 A202 CS01 CS00 A300 A302 A303 A301 A030 CS20 A031 CS21 CS30 CS31 CS11 CS10 A111 A110 A210 A211 A310 A040 A220 A120 A311 F00 A320 F01 A050 F03 F02 A330 F12 A130 F10 F11 F13 A230 F20 F21 B1 B0 K1 F22 F23 K2 K0 F31 F30 F33 F32 K3 K4",
-    "V": "I0 Qm0 QE0 I1 Qm1 I2 QE1 Qm2 H00 Qh00 H02 QE2 H01 Qh02 Qh01 H10 QE3 Qh10 H20 QS0 Qh20 H30 H03 Qh30 QS2 QS1 QS3 H11 Qh03 Qh11 H21 H04 Qh21 H12 H31 Qh12 Qh31 H32 H05 Qh04 H22 Qh32 Qh22 Qh05 Y0 Y1 H23 Y2 H13 B2 Qh13 Qh23 H33 Y3 Qh33 Qy2 Qy1 Qy0 B3 Y4 B4 Qy3 Qy4",
-}
+MOVE_PARTS = [256, 256, 512]
+PIECES = [[256, 256, 256, 256], [512, 512], [512, 512], [512, 256, 256]]
+CHUNKS = [512, 512]
+OPEN_CHUNK = 1
+GROUPS = [(0, 0, 2), (0, 2, 2), (1, 0, 2), (1, 2, 1), (1, 3, 1)]
+WORD_STORES = [[0, 1], [2, 3, 4]]
+RING = 18
+
+SCHEDULE = """
+LE0b LE0a Lmv1 LE1 TE01 Lmv0 TE00 I1 CE01 Lmv2 Qm1 CE00 TE11 LE3 QE0 TE10 I0 CE11 Lmm00 Qm0 M011 I2 CE10 LE2
+M010 A011 M000 QE1 Lmm10 A010 M001 Qm2 A000 M100 M101 H01 Lmm01 A001 M102 Tc A100 TE20 H00 LS1 A101 TE21 Cc
+M103 CE20 M113 Qh01 Lmm20 M110 CE21 A102 M111 M031 Qh00 A103 M030 Lmm30 QE2 TE31 A113 H10 TE30 A030 Lmm11
+M020 A110 M021 M201 A031 Lmm21 TS10 CE31 H03 M112 A111 M200 LS3 CE30 M202 Qh10 A112 M203 Qh03 LS0 QE3 A020
+M213 H11 A021 LS2 M302 A200 M301 A203 M300 Lmm31 A201 TS30 H02 A202 Lw M320 CS10 TS11 H20 CS30 M303 A302
+TS01 A301 M212 A300 Qh11 TS31 A303 TS00 Qh20 CS11 TS21 H30 A213 TS20 CS00 M310 CS01 M311 CS21 QS1 M210 CS31
+M321 QS0 A212 M211 QS3 CS20 Qh30 A210 QS2 A211 Qh02 N02 A321 H21 A311 N03 A320 F02 N00 H32 A310 F03 N01 Qh21
+F00 H31 N11a F01 Qh32 N10a Qh31 Y0 N11 N10 N13a F11 Y1 So0 F10 N13 N12a B0 F13 So1 Y2 B1 U0 N12 Y4 F12 So2
+U1 B2 K0 Y3 U2 K1 So4 B4 B3 K2 So3 U4 Qy0 U3 Qy1 K4 Qy2 K3 Sw0 Qy4 Qy3 Sw1 Ss3 Ss0 Ss1 Ss2
+"""
+ON_VECTOR = ["B0", "B2", "B3", "B4", "CE00", "CE21", "I0", "I1", "I2"]
 
 
 def starts(widths):
-    return [sum(widths[:k]) for k in range(len(widths))]
+    return [sum(widths[:n]) for n in range(len(widths))]
+
+
+def ring_slots(schedule):
+    first = {}
+    cursor = 0
+    for name in schedule:
+        if name[0] == "H":
+            slots = PACK * PIECES[int(name[1])][int(name[2])] // BANK
+            if cursor + slots > RING:
+                cursor = 0
+            first[name] = cursor
+            cursor = cursor + slots
+    return first
 
 
 def tile_fx_member_margin_planes_h3_kernel(
     tc, exposures, moves, margin_map, shares, concentration, addon, scenario_weights, out_0, out_1, out_2
 ):
     nc = tc.nc
-    ORDER = {engine: text.split() for engine, text in ORDER_TEXT.items()}
+    schedule = SCHEDULE.split()
     with ExitStack() as ctx:
         sb = ctx.enter_context(tc.tile_pool(name="sb", bufs=1))
         ps = ctx.enter_context(tc.psum_pool(name="ps", bufs=1))
@@ -54,16 +80,15 @@ def tile_fx_member_margin_planes_h3_kernel(
         def new(name, shape, dtype):
             return sb.tile(shape, dtype, name=name, align_bytes=64)
 
-        banks = [ps.tile([P, BANK], F32, name="bank%d" % b) for b in range(8)]
-        free_banks = list(range(8))
-        bank_of = {}
+        free_banks = [ps.tile([P, BANK], F32, name="bank%d" % b) for b in range(BANKS)]
+        bank = {}
         steps = {}
 
-        def step(name, needs, run, takes_bank=False, frees=None):
-            steps[name] = (needs, run, takes_bank, frees)
+        def step(name, run, takes_bank=False, frees=None):
+            steps[name] = (run, takes_bank, frees)
 
-        def copy_on(name, out, in_):
-            if name in ORDER["V"]:
+        def copy(name, out, in_):
+            if name in ON_VECTOR:
                 nc.vector.tensor_copy(out=out, in_=in_)
             else:
                 nc.scalar.copy(out=out, in_=in_)
@@ -71,47 +96,40 @@ def tile_fx_member_margin_planes_h3_kernel(
         def quantize(codes, scales, grouped):
             nc.vector.quantize_mx(out=codes.bitcast(FP8X4), scales=scales, in_=grouped)
 
+        def multiply(out, lhs_codes, lhs_scales, rhs_codes, rhs_scales, start, stop):
+            nc.tensor.matmul_mx(out=out, lhsT=lhs_codes.bitcast(FP8X4), lhsT_scale=lhs_scales,
+                                rhs=rhs_codes.bitcast(FP8X4), rhs_scale=rhs_scales, start=start, stop=stop)
+
         ident = new("ident", [P, P], F32)
-        vec_rows = new("vec_rows", [8, P], BF16)
-        vec_f32 = new("vec_f32", [P, P], F32)
-        w_row = new("w_row", [P, SCN], BF16)
-        member = new("member", [P, 8], F32)
-
         make_identity(nc, ident[:])
-        nc.gpsimd.memset(vec_f32[:], 0.0)
-        nc.scalar.dma_start(out=vec_rows[0:4, :], in_=concentration.rearrange("(i m) -> i m", m=P))
-        nc.scalar.dma_start(out=vec_rows[4:8, :], in_=addon.rearrange("(i m) -> i m", m=P))
-        nc.scalar.activation(out=vec_f32[0:8, :], in_=vec_rows[:], func=ACT.Identity)
 
-        def turn_member():
-            nc.tensor.transpose(banks[bank_of["Tc"]][:, 0:P], vec_f32[:], ident[:])
+        member_rows = new("member_rows", [2 * TILES, P], BF16)
+        member_square = new("member_square", [P, P], F32)
+        member = new("member", [P, 2 * TILES], F32)
+        nc.gpsimd.memset(member_square[:], 0.0)
+        nc.scalar.dma_start(out=member_rows[0:TILES, :], in_=concentration.rearrange("(i m) -> i m", m=P))
+        nc.scalar.dma_start(out=member_rows[TILES : 2 * TILES, :], in_=addon.rearrange("(i m) -> i m", m=P))
+        nc.scalar.activation(out=member_square[0 : 2 * TILES, :], in_=member_rows[:], func=ACT.Identity)
+        step("Tc", lambda: nc.tensor.transpose(bank["Tc"][:, 0:P], member_square[:], ident[:]), takes_bank=True)
+        step("Cc", lambda: nc.scalar.copy(out=member[:], in_=bank["Tc"][:, 0 : 2 * TILES]), frees="Tc")
 
-        def copy_member():
-            nc.scalar.copy(out=member[:], in_=banks[bank_of["Tc"]][:, 0:8])
+        weights = new("weights", [P, SCN], BF16)
+        step("Lw", lambda: nc.sync.dma_start(out=weights[:], in_=scenario_weights.partition_broadcast(P)))
 
-        step("Tc", [], turn_member, takes_bank=True)
-        step("Cc", ["Tc"], copy_member, frees="Tc")
-        step("Cw", [], lambda: nc.sync.dma_start(out=w_row[:], in_=scenario_weights.partition_broadcast(P)))
-
+        staging = new("staging", [P, PASSES * PACK * BANK], BF16)
         codes = {}
         scales = {}
-        turned = [new("turned%d" % k, [P, 4 * BANK], BF16) for k in range(4)]
 
-        def add_turned_operand(op, g):
-            key = "%s%d" % (op, g)
+        def add_turned_operand(key, g, source):
             raw = new("raw" + key, [P, 4, BANK], BF16)
-            grouped = turned[g]
+            grouped = staging[:, g * PACK * BANK : (g + 1) * PACK * BANK]
             codes[key] = new("codes" + key, [P, BANK], U32)
             scales[key] = new("scales" + key, [P, BANK], U8)
-            if op == "E":
-                source = exposures[BANK * g : BANK * (g + 1), :].rearrange("(m t) k -> m t k", t=4)
+            if "L" + key in schedule:
+                step("L" + key, lambda: nc.sync.dma_start(out=raw[:], in_=source))
             else:
-                source = shares[:, BANK * g : BANK * (g + 1)].rearrange("(i m) k -> m i k", m=P)
-            if key == "E0":
-                step("LE0a", [], lambda: nc.sync.dma_start(out=raw[:, 0:2, :], in_=source[:, 0:2, :]))
-                step("LE0b", [], lambda: nc.sync.dma_start(out=raw[:, 2:4, :], in_=source[:, 2:4, :]))
-            else:
-                step("L" + key, [], lambda: nc.sync.dma_start(out=raw[:], in_=source))
+                step("L%sa" % key, lambda: nc.sync.dma_start(out=raw[:, 0:2, :], in_=source[:, 0:2, :]))
+                step("L%sb" % key, lambda: nc.sync.dma_start(out=raw[:, 2:4, :], in_=source[:, 2:4, :]))
 
             def add_half(h):
                 name = "T%s%d" % (key, h)
@@ -120,273 +138,209 @@ def tile_fx_member_margin_planes_h3_kernel(
                     words = raw[:].bitcast(F32)
                     for j in range(2):
                         for u in range(2):
-                            q = 2 * j + u
-                            nc.tensor.transpose(
-                                banks[bank_of[name]][:, q * P : (q + 1) * P], words[:, 2 * h + j, u:256:2], ident[:]
-                            )
+                            at = (2 * j + u) * P
+                            nc.tensor.transpose(bank[name][:, at : at + P], words[:, 2 * h + j, u : 2 * P : 2], ident[:])
 
-                def copy():
-                    out = grouped[:].bitcast(F32)[:, BANK * h : BANK * (h + 1)]
-                    copy_on("C%s%d" % (key, h), out.rearrange("p (j m u) -> p j m u", j=2, u=2),
-                            banks[bank_of[name]][:].rearrange("p (j u m) -> p j m u", j=2, u=2))
-
-                load = "LE0" + "ab"[h] if key == "E0" else "L" + key
-                step(name, [load], turn, takes_bank=True)
-                step("C%s%d" % (key, h), [name] + (["QE%d" % g] if op == "S" else []), copy, frees=name)
+                out = grouped.bitcast(F32)[:, BANK * h : BANK * (h + 1)].rearrange("p (j m u) -> p j m u", j=2, u=2)
+                step(name, turn, takes_bank=True)
+                step("C" + name[1:], lambda: copy(
+                    "C" + name[1:], out, bank[name][:].rearrange("p (j u m) -> p j m u", j=2, u=2)), frees=name)
 
             add_half(0)
             add_half(1)
-            step("Q" + key, ["C%s0" % key, "C%s1" % key], lambda: quantize(codes[key][:], scales[key][:], grouped[:]))
+            step("Q" + key, lambda: quantize(codes[key][:], scales[key][:], grouped))
 
-        for op in "ES":
-            for g in range(4):
-                add_turned_operand(op, g)
+        for g in range(PASSES):
+            accounts = slice(BANK * g, BANK * (g + 1))
+            add_turned_operand("E%d" % g, g, exposures[accounts, :].rearrange("(m t) k -> m t k", t=PACK))
+            add_turned_operand("S%d" % g, g, shares[:, accounts].rearrange("(i m) k -> m i k", m=P))
 
         move_codes = new("move_codes", [P, SCN], U32)
         move_scales = new("move_scales", [P, SCN], U8)
 
         def add_moves(h, s0, width):
-            raw = new("move_raw%d" % h, [P, 4, width], BF16)
-            grouped = new("move_grouped%d" % h, [P, 4 * width], BF16)
-            source = moves[:, s0 : s0 + width].rearrange("(p t) n -> p t n", t=4)
-            step("Lmv%d" % h, [], lambda: nc.sync.dma_start(out=raw[:], in_=source))
-            step("I%d" % h, ["Lmv%d" % h], lambda: copy_on(
+            raw = new("move_raw%d" % h, [P, PACK, width], BF16)
+            grouped = new("move_grouped%d" % h, [P, PACK * width], BF16)
+            cols = slice(s0, s0 + width)
+            step("Lmv%d" % h, lambda: nc.sync.dma_start(
+                out=raw[:], in_=moves[:, cols].rearrange("(p t) n -> p t n", t=PACK)))
+            step("I%d" % h, lambda: copy(
                 "I%d" % h,
-                grouped[:].rearrange("p (c i t) -> p c t i", i=4, t=4),
-                raw[:].rearrange("p t (c i) -> p c t i", i=4)))
-            step("Qm%d" % h, ["I%d" % h], lambda: quantize(
-                move_codes[:, s0 : s0 + width], move_scales[:, s0 : s0 + width], grouped[:]))
+                grouped[:].rearrange("p (c i t) -> p c t i", i=MOVES_RUN, t=PACK),
+                raw[:].rearrange("p t (c i) -> p c t i", i=MOVES_RUN)))
+            step("Qm%d" % h, lambda: quantize(move_codes[:, cols], move_scales[:, cols], grouped[:]))
 
         for h, (s0, width) in enumerate(zip(starts(MOVE_PARTS), MOVE_PARTS)):
             add_moves(h, s0, width)
 
         maps = {}
 
-        def add_map(g, h):
-            maps[g, h] = new("map%d%d" % (g, h), [P, 4, BANK], BF16)
-            source = margin_map[BANK * g : BANK * (g + 1), BANK * h : BANK * (h + 1)].rearrange("(p t) n -> p t n", t=4)
-            step("Lmm%d%d" % (g, h), [], lambda: nc.sync.dma_start(out=maps[g, h][:], in_=source))
+        def add_map(g, half):
+            maps[g, half] = new("map%d%d" % (g, half), [P, PACK, BANK], BF16)
+            source = margin_map[BANK * g : BANK * (g + 1), BANK * half : BANK * (half + 1)]
+            step("Lmm%d%d" % (g, half), lambda: nc.sync.dma_start(
+                out=maps[g, half][:], in_=source.rearrange("(p t) n -> p t n", t=PACK)))
 
-        for g in range(4):
-            for h in range(2):
-                add_map(g, h)
+        for g in range(PASSES):
+            for half in range(HALVES):
+                add_map(g, half)
 
-        def covering(prefix, widths, s0, width):
-            return [prefix + str(k) for k, (a, w) in enumerate(zip(starts(widths), widths)) if a < s0 + width and a + w > s0]
-
-        h_codes = [new("h_codes%d" % g, [P, SCN], U32) for g in range(4)]
-        h_scales = [new("h_scales%d" % g, [P, SCN], U8) for g in range(4)]
-
-        h_order = [name for name in ORDER["V"] if name[0] == "H"]
-        slot_user = {}
-        size_ring = new("size_ring", [P, ABS_RING * BANK], F32)
-        h_ring = new("h_ring", [P, ABS_RING * BANK], BF16)
-        ring_at = {}
-        ring_needs = {}
-        cursor = 0
-        for name in h_order:
-            nb = 4 * PIECES[int(name[1])][int(name[2])] // BANK
-            if cursor + nb > ABS_RING:
-                cursor = 0
-            ring_at[name] = cursor
-            ring_needs[name] = sorted(set(slot_user[s] for s in range(cursor, cursor + nb) if s in slot_user))
-            for s in range(cursor, cursor + nb):
-                slot_user[s] = name
-            cursor = cursor + nb
+        h_codes = [new("h_codes%d" % g, [P, SCN], U32) for g in range(PASSES)]
+        h_scales = [new("h_scales%d" % g, [P, SCN], U8) for g in range(PASSES)]
+        size_ring = new("size_ring", [P, RING * BANK], F32)
+        h_ring = new("h_ring", [P, RING * BANK], BF16)
+        first_slot = ring_slots(schedule)
 
         def add_piece(g, c, s0, width):
-            nb = 4 * width // BANK
-            per = BANK // width
             key = "%d%d" % (g, c)
-            at = ring_at["H" + key] * BANK
-            size = size_ring[:, at : at + 4 * width]
-            grouped = h_ring[:, at : at + 4 * width]
+            per_bank = BANK // width
+            at = first_slot["H" + key] * BANK
+            size = size_ring[:, at : at + PACK * width]
+            grouped = h_ring[:, at : at + PACK * width]
             cols = slice(s0, s0 + width)
+            half, n0 = divmod(s0, BANK)
 
             def add_bank(b):
                 name = "M%s%d" % (key, b)
 
-                def multiply():
-                    for j in range(per):
-                        t = b * per + j
-                        nc.tensor.matmul_mx(
-                            out=banks[bank_of[name]][:, j * width : (j + 1) * width],
-                            lhsT=codes["E%d" % g][:, t * P : (t + 1) * P].bitcast(FP8X4),
-                            lhsT_scale=scales["E%d" % g][:, t * P : (t + 1) * P],
-                            rhs=move_codes[:, cols].bitcast(FP8X4),
-                            rhs_scale=move_scales[:, cols],
-                            start=True,
-                            stop=True,
-                        )
+                def first_product():
+                    for j in range(per_bank):
+                        t = b * per_bank + j
+                        multiply(bank[name][:, j * width : (j + 1) * width],
+                                 codes["E%d" % g][:, t * P : (t + 1) * P], scales["E%d" % g][:, t * P : (t + 1) * P],
+                                 move_codes[:, cols], move_scales[:, cols], True, True)
 
-                step(name, ["QE%d" % g] + covering("Qm", MOVE_PARTS, s0, width), multiply, takes_bank=True)
-                step("A%s%d" % (key, b), [name] + ring_needs["H" + key], lambda: nc.scalar.activation(
-                    out=size[:, b * BANK : (b + 1) * BANK], in_=banks[bank_of[name]][:], func=ACT.Abs), frees=name)
+                step(name, first_product, takes_bank=True)
+                step("A" + name[1:], lambda: nc.scalar.activation(
+                    out=size[:, b * BANK : (b + 1) * BANK], in_=bank[name][:], func=ACT.Abs), frees=name)
 
-            for b in range(nb):
+            for b in range(PACK // per_bank):
                 add_bank(b)
-            half, n0 = divmod(s0, BANK)
-            step("H" + key,
-                 ["A%s%d" % (key, b) for b in range(nb)] + ["Lmm%d%d" % (g, half)]
-                 + ["Qh" + u[1:] for u in ring_needs["H" + key]],
-                 lambda: nc.vector.tensor_tensor(
-                     out=grouped.rearrange("p (c i t) -> p c t i", i=RUN, t=4),
-                     in0=size.rearrange("p (t c i) -> p c t i", i=RUN, t=4),
-                     in1=maps[g, half][:, :, n0 : n0 + width].rearrange("p t (c i) -> p c t i", i=RUN),
-                     op=MULT))
-            step("Qh" + key, ["H" + key], lambda: quantize(h_codes[g][:, cols], h_scales[g][:, cols], grouped))
+            step("H" + key, lambda: nc.vector.tensor_tensor(
+                out=grouped.rearrange("p (c i t) -> p c t i", i=H_RUN, t=PACK),
+                in0=size.rearrange("p (t c i) -> p c t i", i=H_RUN, t=PACK),
+                in1=maps[g, half][:, :, n0 : n0 + width].rearrange("p t (c i) -> p c t i", i=H_RUN),
+                op=MULT))
+            step("Qh" + key, lambda: quantize(h_codes[g][:, cols], h_scales[g][:, cols], grouped))
 
-        for g in range(4):
+        for g in range(PASSES):
             for c, (s0, width) in enumerate(zip(starts(PIECES[g]), PIECES[g])):
                 add_piece(g, c, s0, width)
 
-        y = new("y", [P, 8, 4, P], F32)
-        y_codes = new("y_codes", [P, SCN], U32)
-        y_scales = new("y_scales", [P, SCN], U8)
+        y = new("y", [P, HALVES, TILES, BANK], F32)
+        y_codes = new("y_codes", [P, HALVES, MEM], U32)
+        y_scales = new("y_scales", [P, HALVES, MEM], U8)
 
         def add_chunk(c, s0, width):
-            nb = 4 * width // BANK
-            per = BANK // width
+            per_bank = BANK // width
             cols = slice(s0, s0 + width)
 
-            def ready(g):
-                return covering("Qh%d" % g, PIECES[g], s0, width) + ["QS%d" % g]
+            def second_product(owner, j, i, passes):
+                for g in passes:
+                    multiply(bank[owner][:, j * width : (j + 1) * width],
+                             codes["S%d" % g][:, i * P : (i + 1) * P], scales["S%d" % g][:, i * P : (i + 1) * P],
+                             h_codes[g][:, cols], h_scales[g][:, cols], g == 0, g == PASSES - 1)
 
-            def passes(owner, j, i, groups):
-                for g in groups:
-                    nc.tensor.matmul_mx(
-                        out=banks[bank_of[owner]][:, j * width : (j + 1) * width],
-                        lhsT=codes["S%d" % g][:, i * P : (i + 1) * P].bitcast(FP8X4),
-                        lhsT_scale=scales["S%d" % g][:, i * P : (i + 1) * P],
-                        rhs=h_codes[g][:, cols].bitcast(FP8X4),
-                        rhs_scale=h_scales[g][:, cols],
-                        start=(g == 0),
-                        stop=(g == 3),
-                    )
-
-            def add_affine(owner, needs, j, i, frees):
+            def add_affine(owner, j, i, frees):
                 name = "F%d%d" % (c, i)
-                out = y[:, s0 // P : (s0 + width) // P, i, :]
+                out = y[:, s0 // BANK, i, s0 % BANK : s0 % BANK + width]
+                factor = member[:, i : i + 1]
+                offset = member[:, TILES + i : TILES + i + 1]
 
                 def run():
-                    in_ = banks[bank_of[owner]][:, j * width : (j + 1) * width].rearrange("p (k n) -> p k n", n=P)
-                    if name in ORDER["V"]:
-                        nc.vector.tensor_scalar(out=out, in0=in_, scalar1=member[:, i : i + 1],
-                                                scalar2=member[:, 4 + i : 5 + i], op0=MULT, op1=ADD)
+                    in_ = bank[owner][:, j * width : (j + 1) * width]
+                    if name in ON_VECTOR:
+                        nc.vector.tensor_scalar(out=out, in0=in_, scalar1=factor, scalar2=offset, op0=MULT, op1=ADD)
                     else:
-                        nc.scalar.activation(out=out, in_=in_, func=ACT.Identity,
-                                             scale=member[:, i : i + 1], bias=member[:, 4 + i : 5 + i])
+                        nc.scalar.activation(out=out, in_=in_, func=ACT.Identity, scale=factor, bias=offset)
 
-                step(name, needs + ["Cc"], run, frees=frees)
+                step(name, run, frees=frees)
 
-            def add_open_group(i):
+            def add_open_sum(i):
                 owner = "N%d%da" % (c, i)
-                step(owner, ready(0) + ready(1) + ready(2), lambda: passes(owner, 0, i, range(3)), takes_bank=True)
-                step(owner[:-1], [owner] + ready(3), lambda: passes(owner, 0, i, [3]))
-                add_affine(owner, [owner[:-1]], 0, i, owner)
+                step(owner, lambda: second_product(owner, 0, i, range(PASSES - 1)), takes_bank=True)
+                step(owner[:-1], lambda: second_product(owner, 0, i, [PASSES - 1]))
+                add_affine(owner, 0, i, owner)
 
-            def add_closed_groups(b):
+            def add_closed_sums(b):
                 owner = "N%d%d" % (c, b)
 
                 def run():
-                    for j in range(per):
-                        passes(owner, j, b * per + j, range(4))
+                    for j in range(per_bank):
+                        second_product(owner, j, b * per_bank + j, range(PASSES))
 
-                step(owner, ready(0) + ready(1) + ready(2) + ready(3), run, takes_bank=True)
-                names = [name for name in ORDER["A"] + ORDER["V"]
-                         if name in ["F%d%d" % (c, b * per + j) for j in range(per)]]
-                for j in range(per):
-                    i = b * per + j
-                    is_last = names[-1] == "F%d%d" % (c, i)
-                    add_affine(owner, [owner] + (names[:-1] if is_last else []), j, i, owner if is_last else None)
+                step(owner, run, takes_bank=True)
+                for j in range(per_bank):
+                    add_affine(owner, j, b * per_bank + j, owner if j == per_bank - 1 else None)
 
-            if c in OPEN_CHUNKS:
-                for i in range(4):
-                    add_open_group(i)
+            if c == OPEN_CHUNK:
+                for i in range(TILES):
+                    add_open_sum(i)
             else:
-                for b in range(nb):
-                    add_closed_groups(b)
+                for b in range(TILES // per_bank):
+                    add_closed_sums(b)
 
         for c, (s0, width) in enumerate(zip(starts(CHUNKS), CHUNKS)):
             add_chunk(c, s0, width)
 
-        def add_group(e, k0, n):
-            part = y[:, k0 : k0 + n, :, :]
-            rounded = new("rounded%d" % e, [P, n * BANK], BF16)
-            grouped = new("y_grouped%d" % e, [P, n * BANK], BF16)
-            cols = slice(k0 * P, (k0 + n) * P)
+        def add_group(e, half, i0, n):
+            cols = slice(half * BANK, (half + 1) * BANK)
+            members = slice(i0 * P, (i0 + n) * P)
+            part = y[:, half, i0 : i0 + n, :]
+            at = 2 * (half * TILES + i0) * BANK
+            rounded = staging[:, at : at + n * BANK]
+            grouped = staging[:, at + n * BANK : at + 2 * n * BANK]
             name = "U%d" % e
-            weights = w_row[:, cols].rearrange("p (k n) -> p k n", n=P).unsqueeze(2).to_broadcast([P, n, 4, P])
+            spread = weights[:, cols].unsqueeze(1).to_broadcast([P, n, BANK])
 
             def turn():
-                words = rounded[:].bitcast(F32).rearrange("p (u k j) -> p u k j", u=2, j=P)
-                for k in range(n):
+                words = rounded.bitcast(F32).rearrange("p (u i j) -> p u i j", u=2, j=P)
+                for i in range(n):
                     for u in range(2):
-                        q = 2 * k + u
-                        nc.tensor.transpose(banks[bank_of[name]][:, q * P : (q + 1) * P], words[:, u, k, :], ident[:])
+                        to = (2 * i + u) * P
+                        nc.tensor.transpose(bank[name][:, to : to + P], words[:, u, i, :], ident[:])
 
-            affine = [f + str(i) for f in covering("F", CHUNKS, k0 * P, n * P) for i in range(4)]
-            step("Y%d" % e, affine + ["Cw"], lambda: nc.vector.tensor_tensor(out=part, in0=part, in1=weights, op=MULT))
-            step("B%d" % e, ["Y%d" % e], lambda: copy_on(
+            step("Y%d" % e, lambda: nc.vector.tensor_tensor(out=part, in0=part, in1=spread, op=MULT))
+            step("So%d" % e, lambda: nc.sync.dma_start(
+                out=out_0[members, cols].rearrange("(i m) s -> m i s", m=P), in_=part))
+            step("B%d" % e, lambda: copy(
                 "B%d" % e,
-                rounded[:].rearrange("p (u j e) -> p u j e", u=2, e=2),
-                part.rearrange("p k i (j u e) -> p u (k i j) e", u=2, e=2)))
-            step(name, ["B%d" % e], turn, takes_bank=True)
-            step("K%d" % e, [name], lambda: copy_on(
+                rounded.rearrange("p (u j e) -> p u j e", u=2, e=2),
+                part.rearrange("p i (j u e) -> p u (i j) e", u=2, e=2)))
+            step(name, turn, takes_bank=True)
+            step("K%d" % e, lambda: copy(
                 "K%d" % e,
-                grouped[:].bitcast(F32).rearrange("p (k m u) -> p k m u", u=2, m=P),
-                banks[bank_of[name]][:, 0 : n * 2 * P].rearrange("p (k u m) -> p k m u", u=2, m=P)), frees=name)
-            step("Qy%d" % e, ["K%d" % e], lambda: quantize(y_codes[:, cols], y_scales[:, cols], grouped[:]))
+                grouped.bitcast(F32).rearrange("p (i m u) -> p i m u", u=2, m=P),
+                bank[name][:, 0 : 2 * n * P].rearrange("p (i u m) -> p i m u", u=2, m=P)), frees=name)
+            step("Qy%d" % e, lambda: quantize(y_codes[:, half, members], y_scales[:, half, members], grouped))
 
-            def add_store(k):
-                step("So%d" % k, ["Y%d" % e], lambda: nc.sync.dma_start(
-                    out=out_0[:, k * P : (k + 1) * P].rearrange("(i m) s -> m i s", m=P), in_=y[:, k, :, :]))
+        for e, (half, i0, n) in enumerate(GROUPS):
+            add_group(e, half, i0, n)
 
-            for k in range(k0, k0 + n):
-                add_store(k)
+        out_words = out_1.rearrange("g p m t -> p g (m t)").bitcast(I32)
+        out_scales = out_2.rearrange("g q m -> q g m").bitcast(I32)
 
-        for e, (k0, n) in enumerate(zip(starts(GROUPS), GROUPS)):
-            add_group(e, k0, n)
+        def add_word_store(b, groups):
+            half, i0, n = GROUPS[groups[0]]
+            members = slice(i0 * P, (i0 + sum(GROUPS[e][2] for e in groups)) * P)
+            step("Sw%d" % b, lambda: nc.sync.dma_start(
+                out=out_words[:, half, members], in_=y_codes[:, half, members].bitcast(I32)))
 
-        out_words = out_1.rearrange("g (c j) (i m) t -> j i (g c) (m t)", j=32, m=P).bitcast(I32)
-        out_scales = out_2.rearrange("g (c r) (i m) -> r i (g c) m", r=4, m=P).bitcast(I32)
+        def add_scale_store(q):
+            step("Ss%d" % q, lambda: nc.scalar.dma_start(
+                out=out_scales[4 * q : 4 * q + 4, :, :],
+                in_=y_scales[QUADRANT * q : QUADRANT * q + 4, :, :].bitcast(I32)))
 
-        def add_word_store(b, groups, i):
-            k0 = starts(GROUPS)[groups[0]]
-            k1 = k0 + sum(GROUPS[e] for e in groups)
-            step("Sw%d%d" % (b, i), ["Qy%d" % e for e in groups], lambda: nc.sync.dma_start(
-                out=out_words[:, i, k0:k1, :],
-                in_=y_codes[32 * i : 32 * i + 32, k0 * P : k1 * P].bitcast(I32).rearrange("p (k m) -> p k m", m=P)))
+        for b, groups in enumerate(WORD_STORES):
+            add_word_store(b, groups)
+        for q in range(P // QUADRANT):
+            add_scale_store(q)
 
-        def add_scale_store(i):
-            step("Ss%d" % i, ["Qy%d" % e for e in range(len(GROUPS))] + ORDER["A"][-1:], lambda: nc.scalar.dma_start(
-                out=out_scales[:, i, :, :],
-                in_=y_scales[32 * i : 32 * i + 4, :].bitcast(I32).rearrange("p (k m) -> p k m", m=P // 4)))
-
-        for i in range(4):
-            for b, groups in enumerate(WORD_BATCHES):
-                add_word_store(b, groups, i)
-            add_scale_store(i)
-
-        done = set()
-        at = {engine: 0 for engine in ORDER}
-        assert sorted(steps) == sorted(name for names in ORDER.values() for name in names)
-        while len(done) < len(steps):
-            moved = False
-            for engine in "DPVA":
-                if at[engine] == len(ORDER[engine]):
-                    continue
-                name = ORDER[engine][at[engine]]
-                needs, run, takes_bank, frees = steps[name]
-                if not all(need in done for need in needs) or (takes_bank and not free_banks):
-                    continue
-                if takes_bank:
-                    bank_of[name] = free_banks.pop(0)
-                run()
-                if frees:
-                    free_banks.append(bank_of[frees])
-                done.add(name)
-                at[engine] = at[engine] + 1
-                moved = True
-                break
-            assert moved
+        assert sorted(steps) == sorted(schedule)
+        for name in schedule:
+            run, takes_bank, frees = steps[name]
+            if takes_bank:
+                bank[name] = free_banks.pop(0)
+            run()
+            if frees:
+                free_banks.append(bank[frees])

from contextlib import ExitStack

import concourse.mybir as mybir
from concourse.masks import make_identity

F32 = mybir.dt.float32
BF16 = mybir.dt.bfloat16
U32 = mybir.dt.uint32
I32 = mybir.dt.int32
U8 = mybir.dt.uint8
FP8X4 = mybir.dt.float8_e4m3fn_x4
ACT = mybir.ActivationFunctionType
MULT = mybir.AluOpType.mult
ADD = mybir.AluOpType.add

ACC, CUR, SCN, MEM = 2048, 512, 1024, 512
FLOPS = 2 * ACC * CUR * SCN + 2 * MEM * ACC * SCN

P = 128
PACK = 4
BANK = 512
BANKS = 8
PASSES = ACC // BANK
TILES = MEM // P
HALVES = SCN // BANK
QUADRANT = 32

H_RUN = 2
MOVES_RUN = 4

MOVE_PARTS = [256, 256, 512]
PIECES = [[256, 256, 256, 256], [512, 512], [512, 512], [512, 256, 256]]
CHUNKS = [512, 512]
OPEN_CHUNK = 1
GROUPS = [(0, 0, 2), (0, 2, 2), (1, 0, 2), (1, 2, 1), (1, 3, 1)]
WORD_STORES = [[0, 1], [2, 3, 4]]
RING = 18

SCHEDULE = """
LE0b LE0a Lmv1 LE1 TE01 Lmv0 TE00 I1 CE01 Lmv2 Qm1 CE00 TE11 LE3 QE0 TE10 I0 CE11 Lmm00 Qm0 M011 I2 CE10 LE2
M010 A011 M000 QE1 Lmm10 A010 M001 Qm2 A000 M100 M101 H01 Lmm01 A001 M102 Tc A100 TE20 H00 LS1 A101 TE21 Cc
M103 CE20 M113 Qh01 Lmm20 M110 CE21 A102 M111 M031 Qh00 A103 M030 Lmm30 QE2 TE31 A113 H10 TE30 A030 Lmm11
M020 A110 M021 M201 A031 Lmm21 TS10 CE31 H03 M112 A111 M200 LS3 CE30 M202 Qh10 A112 M203 Qh03 LS0 QE3 A020
M213 H11 A021 LS2 M302 A200 M301 A203 M300 Lmm31 A201 TS30 H02 A202 Lw M320 CS10 TS11 H20 CS30 M303 A302
TS01 A301 M212 A300 Qh11 TS31 A303 TS00 Qh20 CS11 TS21 H30 A213 TS20 CS00 M310 CS01 M311 CS21 QS1 M210 CS31
M321 QS0 A212 M211 QS3 CS20 Qh30 A210 QS2 A211 Qh02 N02 A321 H21 A311 N03 A320 F02 N00 H32 A310 F03 N01 Qh21
F00 H31 N11a F01 Qh32 N10a Qh31 Y0 N11 N10 N13a F11 Y1 So0 F10 N13 N12a B0 F13 So1 Y2 B1 U0 N12 Y4 F12 So2
U1 B2 K0 Y3 U2 K1 So4 B4 B3 K2 So3 U4 Qy0 U3 Qy1 K4 Qy2 K3 Sw0 Qy4 Qy3 Sw1 Ss3 Ss0 Ss1 Ss2
"""
ON_VECTOR = ["B0", "B2", "B3", "B4", "CE00", "CE21", "I0", "I1", "I2"]


def starts(widths):
    return [sum(widths[:n]) for n in range(len(widths))]


def ring_slots(schedule):
    first = {}
    cursor = 0
    for name in schedule:
        if name[0] == "H":
            slots = PACK * PIECES[int(name[1])][int(name[2])] // BANK
            if cursor + slots > RING:
                cursor = 0
            first[name] = cursor
            cursor = cursor + slots
    return first


def tile_fx_member_margin_planes_h3_kernel(
    tc, exposures, moves, margin_map, shares, concentration, addon, scenario_weights, out_0, out_1, out_2
):
    nc = tc.nc
    schedule = SCHEDULE.split()
    with ExitStack() as ctx:
        sb = ctx.enter_context(tc.tile_pool(name="sb", bufs=1))
        ps = ctx.enter_context(tc.psum_pool(name="ps", bufs=1))
        ctx.enter_context(tc.manual_schedule())

        def new(name, shape, dtype):
            return sb.tile(shape, dtype, name=name, align_bytes=64)

        free_banks = [ps.tile([P, BANK], F32, name="bank%d" % b) for b in range(BANKS)]
        bank = {}
        steps = {}

        def step(name, run, takes_bank=False, frees=None):
            steps[name] = (run, takes_bank, frees)

        def copy(name, out, in_):
            if name in ON_VECTOR:
                nc.vector.tensor_copy(out=out, in_=in_)
            else:
                nc.scalar.copy(out=out, in_=in_)

        def quantize(codes, scales, grouped):
            nc.vector.quantize_mx(out=codes.bitcast(FP8X4), scales=scales, in_=grouped)

        def multiply(out, lhs_codes, lhs_scales, rhs_codes, rhs_scales, start, stop):
            nc.tensor.matmul_mx(out=out, lhsT=lhs_codes.bitcast(FP8X4), lhsT_scale=lhs_scales,
                                rhs=rhs_codes.bitcast(FP8X4), rhs_scale=rhs_scales, start=start, stop=stop)

        ident = new("ident", [P, P], F32)
        make_identity(nc, ident[:])

        member_rows = new("member_rows", [2 * TILES, P], BF16)
        member_square = new("member_square", [P, P], F32)
        member = new("member", [P, 2 * TILES], F32)
        nc.gpsimd.memset(member_square[:], 0.0)
        nc.scalar.dma_start(out=member_rows[0:TILES, :], in_=concentration.rearrange("(i m) -> i m", m=P))
        nc.scalar.dma_start(out=member_rows[TILES : 2 * TILES, :], in_=addon.rearrange("(i m) -> i m", m=P))
        nc.scalar.activation(out=member_square[0 : 2 * TILES, :], in_=member_rows[:], func=ACT.Identity)
        step("Tc", lambda: nc.tensor.transpose(bank["Tc"][:, 0:P], member_square[:], ident[:]), takes_bank=True)
        step("Cc", lambda: nc.scalar.copy(out=member[:], in_=bank["Tc"][:, 0 : 2 * TILES]), frees="Tc")

        weights = new("weights", [P, SCN], BF16)
        step("Lw", lambda: nc.sync.dma_start(out=weights[:], in_=scenario_weights.partition_broadcast(P)))

        staging = new("staging", [P, PASSES * PACK * BANK], BF16)
        codes = {}
        scales = {}

        def add_turned_operand(key, g, source):
            raw = new("raw" + key, [P, 4, BANK], BF16)
            grouped = staging[:, g * PACK * BANK : (g + 1) * PACK * BANK]
            codes[key] = new("codes" + key, [P, BANK], U32)
            scales[key] = new("scales" + key, [P, BANK], U8)
            if "L" + key in schedule:
                step("L" + key, lambda: nc.sync.dma_start(out=raw[:], in_=source))
            else:
                step("L%sa" % key, lambda: nc.sync.dma_start(out=raw[:, 0:2, :], in_=source[:, 0:2, :]))
                step("L%sb" % key, lambda: nc.sync.dma_start(out=raw[:, 2:4, :], in_=source[:, 2:4, :]))

            def add_half(h):
                name = "T%s%d" % (key, h)

                def turn():
                    words = raw[:].bitcast(F32)
                    for j in range(2):
                        for u in range(2):
                            at = (2 * j + u) * P
                            nc.tensor.transpose(bank[name][:, at : at + P], words[:, 2 * h + j, u : 2 * P : 2], ident[:])

                out = grouped.bitcast(F32)[:, BANK * h : BANK * (h + 1)].rearrange("p (j m u) -> p j m u", j=2, u=2)
                step(name, turn, takes_bank=True)
                step("C" + name[1:], lambda: copy(
                    "C" + name[1:], out, bank[name][:].rearrange("p (j u m) -> p j m u", j=2, u=2)), frees=name)

            add_half(0)
            add_half(1)
            step("Q" + key, lambda: quantize(codes[key][:], scales[key][:], grouped))

        for g in range(PASSES):
            accounts = slice(BANK * g, BANK * (g + 1))
            add_turned_operand("E%d" % g, g, exposures[accounts, :].rearrange("(m t) k -> m t k", t=PACK))
            add_turned_operand("S%d" % g, g, shares[:, accounts].rearrange("(i m) k -> m i k", m=P))

        move_codes = new("move_codes", [P, SCN], U32)
        move_scales = new("move_scales", [P, SCN], U8)

        def add_moves(h, s0, width):
            raw = new("move_raw%d" % h, [P, PACK, width], BF16)
            grouped = new("move_grouped%d" % h, [P, PACK * width], BF16)
            cols = slice(s0, s0 + width)
            step("Lmv%d" % h, lambda: nc.sync.dma_start(
                out=raw[:], in_=moves[:, cols].rearrange("(p t) n -> p t n", t=PACK)))
            step("I%d" % h, lambda: copy(
                "I%d" % h,
                grouped[:].rearrange("p (c i t) -> p c t i", i=MOVES_RUN, t=PACK),
                raw[:].rearrange("p t (c i) -> p c t i", i=MOVES_RUN)))
            step("Qm%d" % h, lambda: quantize(move_codes[:, cols], move_scales[:, cols], grouped[:]))

        for h, (s0, width) in enumerate(zip(starts(MOVE_PARTS), MOVE_PARTS)):
            add_moves(h, s0, width)

        maps = {}

        def add_map(g, half):
            maps[g, half] = new("map%d%d" % (g, half), [P, PACK, BANK], BF16)
            source = margin_map[BANK * g : BANK * (g + 1), BANK * half : BANK * (half + 1)]
            step("Lmm%d%d" % (g, half), lambda: nc.sync.dma_start(
                out=maps[g, half][:], in_=source.rearrange("(p t) n -> p t n", t=PACK)))

        for g in range(PASSES):
            for half in range(HALVES):
                add_map(g, half)

        h_codes = [new("h_codes%d" % g, [P, SCN], U32) for g in range(PASSES)]
        h_scales = [new("h_scales%d" % g, [P, SCN], U8) for g in range(PASSES)]
        size_ring = new("size_ring", [P, RING * BANK], F32)
        h_ring = new("h_ring", [P, RING * BANK], BF16)
        first_slot = ring_slots(schedule)

        def add_piece(g, c, s0, width):
            key = "%d%d" % (g, c)
            per_bank = BANK // width
            at = first_slot["H" + key] * BANK
            size = size_ring[:, at : at + PACK * width]
            grouped = h_ring[:, at : at + PACK * width]
            cols = slice(s0, s0 + width)
            half, n0 = divmod(s0, BANK)

            def add_bank(b):
                name = "M%s%d" % (key, b)

                def first_product():
                    for j in range(per_bank):
                        t = b * per_bank + j
                        multiply(bank[name][:, j * width : (j + 1) * width],
                                 codes["E%d" % g][:, t * P : (t + 1) * P], scales["E%d" % g][:, t * P : (t + 1) * P],
                                 move_codes[:, cols], move_scales[:, cols], True, True)

                step(name, first_product, takes_bank=True)
                step("A" + name[1:], lambda: nc.scalar.activation(
                    out=size[:, b * BANK : (b + 1) * BANK], in_=bank[name][:], func=ACT.Abs), frees=name)

            for b in range(PACK // per_bank):
                add_bank(b)
            step("H" + key, lambda: nc.vector.tensor_tensor(
                out=grouped.rearrange("p (c i t) -> p c t i", i=H_RUN, t=PACK),
                in0=size.rearrange("p (t c i) -> p c t i", i=H_RUN, t=PACK),
                in1=maps[g, half][:, :, n0 : n0 + width].rearrange("p t (c i) -> p c t i", i=H_RUN),
                op=MULT))
            step("Qh" + key, lambda: quantize(h_codes[g][:, cols], h_scales[g][:, cols], grouped))

        for g in range(PASSES):
            for c, (s0, width) in enumerate(zip(starts(PIECES[g]), PIECES[g])):
                add_piece(g, c, s0, width)

        y = new("y", [P, HALVES, TILES, BANK], F32)
        y_codes = new("y_codes", [P, HALVES, MEM], U32)
        y_scales = new("y_scales", [P, HALVES, MEM], U8)

        def add_chunk(c, s0, width):
            per_bank = BANK // width
            cols = slice(s0, s0 + width)

            def second_product(owner, j, i, passes):
                for g in passes:
                    multiply(bank[owner][:, j * width : (j + 1) * width],
                             codes["S%d" % g][:, i * P : (i + 1) * P], scales["S%d" % g][:, i * P : (i + 1) * P],
                             h_codes[g][:, cols], h_scales[g][:, cols], g == 0, g == PASSES - 1)

            def add_affine(owner, j, i, frees):
                name = "F%d%d" % (c, i)
                out = y[:, s0 // BANK, i, s0 % BANK : s0 % BANK + width]
                factor = member[:, i : i + 1]
                offset = member[:, TILES + i : TILES + i + 1]

                def run():
                    in_ = bank[owner][:, j * width : (j + 1) * width]
                    if name in ON_VECTOR:
                        nc.vector.tensor_scalar(out=out, in0=in_, scalar1=factor, scalar2=offset, op0=MULT, op1=ADD)
                    else:
                        nc.scalar.activation(out=out, in_=in_, func=ACT.Identity, scale=factor, bias=offset)

                step(name, run, frees=frees)

            def add_open_sum(i):
                owner = "N%d%da" % (c, i)
                step(owner, lambda: second_product(owner, 0, i, range(PASSES - 1)), takes_bank=True)
                step(owner[:-1], lambda: second_product(owner, 0, i, [PASSES - 1]))
                add_affine(owner, 0, i, owner)

            def add_closed_sums(b):
                owner = "N%d%d" % (c, b)

                def run():
                    for j in range(per_bank):
                        second_product(owner, j, b * per_bank + j, range(PASSES))

                step(owner, run, takes_bank=True)
                for j in range(per_bank):
                    add_affine(owner, j, b * per_bank + j, owner if j == per_bank - 1 else None)

            if c == OPEN_CHUNK:
                for i in range(TILES):
                    add_open_sum(i)
            else:
                for b in range(TILES // per_bank):
                    add_closed_sums(b)

        for c, (s0, width) in enumerate(zip(starts(CHUNKS), CHUNKS)):
            add_chunk(c, s0, width)

        def add_group(e, half, i0, n):
            cols = slice(half * BANK, (half + 1) * BANK)
            members = slice(i0 * P, (i0 + n) * P)
            part = y[:, half, i0 : i0 + n, :]
            at = 2 * (half * TILES + i0) * BANK
            rounded = staging[:, at : at + n * BANK]
            grouped = staging[:, at + n * BANK : at + 2 * n * BANK]
            name = "U%d" % e
            spread = weights[:, cols].unsqueeze(1).to_broadcast([P, n, BANK])

            def turn():
                words = rounded.bitcast(F32).rearrange("p (u i j) -> p u i j", u=2, j=P)
                for i in range(n):
                    for u in range(2):
                        to = (2 * i + u) * P
                        nc.tensor.transpose(bank[name][:, to : to + P], words[:, u, i, :], ident[:])

            step("Y%d" % e, lambda: nc.vector.tensor_tensor(out=part, in0=part, in1=spread, op=MULT))
            step("So%d" % e, lambda: nc.sync.dma_start(
                out=out_0[members, cols].rearrange("(i m) s -> m i s", m=P), in_=part))
            step("B%d" % e, lambda: copy(
                "B%d" % e,
                rounded.rearrange("p (u j e) -> p u j e", u=2, e=2),
                part.rearrange("p i (j u e) -> p u (i j) e", u=2, e=2)))
            step(name, turn, takes_bank=True)
            step("K%d" % e, lambda: copy(
                "K%d" % e,
                grouped.bitcast(F32).rearrange("p (i m u) -> p i m u", u=2, m=P),
                bank[name][:, 0 : 2 * n * P].rearrange("p (i u m) -> p i m u", u=2, m=P)), frees=name)
            step("Qy%d" % e, lambda: quantize(y_codes[:, half, members], y_scales[:, half, members], grouped))

        for e, (half, i0, n) in enumerate(GROUPS):
            add_group(e, half, i0, n)

        out_words = out_1.rearrange("g p m t -> p g (m t)").bitcast(I32)
        out_scales = out_2.rearrange("g q m -> q g m").bitcast(I32)

        def add_word_store(b, groups):
            half, i0, n = GROUPS[groups[0]]
            members = slice(i0 * P, (i0 + sum(GROUPS[e][2] for e in groups)) * P)
            step("Sw%d" % b, lambda: nc.sync.dma_start(
                out=out_words[:, half, members], in_=y_codes[:, half, members].bitcast(I32)))

        def add_scale_store(q):
            step("Ss%d" % q, lambda: nc.scalar.dma_start(
                out=out_scales[4 * q : 4 * q + 4, :, :],
                in_=y_scales[QUADRANT * q : QUADRANT * q + 4, :, :].bitcast(I32)))

        for b, groups in enumerate(WORD_STORES):
            add_word_store(b, groups)
        for q in range(P // QUADRANT):
            add_scale_store(q)

        assert sorted(steps) == sorted(schedule)
        for name in schedule:
            run, takes_bank, frees = steps[name]
            if takes_bank:
                bank[name] = free_banks.pop(0)
            run()
            if frees:
                free_banks.append(bank[frees])
